import numpy as np
import ml_dtypes


def mxq(x, axis, fmt="e4m3"):
    dtype, down = {"e4m3": (ml_dtypes.float8_e4m3fn, 7), "e5m2": (ml_dtypes.float8_e5m2, 14)}[fmt]
    v = np.moveaxis(np.asarray(x, np.float32).astype(ml_dtypes.bfloat16).astype(np.float64), axis, -1)
    blocks = v.reshape(v.shape[:-1] + (-1, 32))
    amax = np.abs(blocks).max(-1, keepdims=True)
    byte = np.maximum(np.where(amax > 0, np.frexp(amax)[1] - 1 + 127, 0) - down, 1)
    scale = np.exp2(byte - 127.0)
    codes = (blocks / scale).astype(np.float32).astype(dtype).astype(np.float64)
    return np.moveaxis((codes * scale).reshape(v.shape), -1, axis)


WIDE = False


def mx_kscale(k):
    if not WIDE:
        return np.ones(k)
    levels = np.array([30, -30])
    if k % 512:
        return np.exp2(np.random.permutation(np.resize(levels, k // 32))).repeat(32)
    a = np.empty((k // 512, 16))
    for p in range(k // 512):
        a[p, :8] = np.random.permutation(np.resize(levels, 8))
        for g in range(8):
            far = levels[np.abs(levels - a[p, g]) >= 10]
            a[p, g + 8] = far[np.random.randint(len(far))]
    return np.exp2(a.ravel()).repeat(32)


BF16 = ml_dtypes.bfloat16


def bf(x):
    return np.asarray(x, np.float32).astype(BF16)


def f64(x):
    return np.asarray(x).astype(np.float64)


E2M1 = np.array([0.0, 0.5, 1.0, 1.5, 2.0, 3.0, 4.0, 6.0, -0.0, -0.5, -1.0, -1.5, -2.0, -3.0, -4.0, -6.0])


def pack_weight(w, fmt):
    k, n = w.shape
    w = f64(bf(w)).reshape(k // 32, 32, n)
    amax = np.abs(w).max(1)
    if fmt == "e4m3":
        byte = np.frexp(amax)[1] - 1 + 127 - 7
    else:
        mant, ex = np.frexp(amax / 6.0)
        byte = np.where(mant > 0.5, ex, ex - 1) + 127
    byte = np.clip(np.where(amax > 0, byte, 1), 1, 254)
    scaled = (w * np.exp2(127.0 - byte)[:, None, :]).reshape(k, n).astype(np.float32)
    by_word = np.ascontiguousarray(scaled.reshape(k // 512, 128, 4, n).transpose(0, 1, 3, 2))
    if fmt == "e4m3":
        words = by_word.astype(ml_dtypes.float8_e4m3fn).view(np.uint8)
    else:
        c = by_word.astype(ml_dtypes.float4_e2m1fn).view(np.uint8) & 0xF
        words = c[..., 0::2] | (c[..., 1::2] << 4)
    return np.ascontiguousarray(words), np.ascontiguousarray(byte.astype(np.uint8).reshape(k // 512, 16, n))


def unpack_weight(words, scales, fmt):
    g, p, n, _ = words.shape
    if fmt == "e4m3":
        vals = np.ascontiguousarray(words).view(ml_dtypes.float8_e4m3fn).astype(np.float64)
    else:
        nib = np.empty((g, p, n, 4), np.uint8)
        nib[..., 0::2] = words & 0xF
        nib[..., 1::2] = words >> 4
        vals = E2M1[nib]
    vals = vals * np.repeat(np.exp2(scales.astype(np.float64) - 127.0), 8, axis=1)[..., None]
    return vals.transpose(0, 1, 3, 2).reshape(g * 512, n)
def pack4(w):
    words, scales = pack_weight(w, "e2m1")
    return words.reshape(words.shape[0], 128, -1), scales


def unpack4(words, scales):
    return unpack_weight(words.reshape(words.shape[0], 128, -1, 2), scales, "e2m1")


M, K, N = 512, 1024, 2048


def setup_inputs():
    s = mx_kscale(K)
    t = mx_kscale(N)
    u = np.random.standard_normal((M, K))
    gain = (1 + 0.1 * np.random.standard_normal(K)) * s
    w = np.random.standard_normal((K, N)) / np.sqrt(K) / s[:, None] / t
    c = (1 + 0.1 * np.random.standard_normal(N)) * t
    teacher = np.random.standard_normal((K, N)) / np.sqrt(K) / s[:, None]
    words, scales = pack4(teacher)
    return {"u": bf(u), "gain": bf(gain), "w": bf(w), "c": bf(c),
            "teacher_words": words, "teacher_scales": scales}


def reference(u, gain, w, c, teacher_words, teacher_scales):
    gain, w, c = f64(gain), f64(w), f64(c)
    x = mxq(f64(u) * gain, 1, "e4m3")
    zt = x @ unpack4(teacher_words, teacher_scales)
    zs = (x @ mxq(w, 0, "e4m3")) * c
    d = (zs - zt) * c
    dx = mxq(d, 1, "e5m2") @ mxq(w, 1, "e4m3").T
    du = dx * gain
    return zs, zt, du

@@ -1,0 +1,368 @@
+from contextlib import ExitStack
+
+import concourse.mybir as mybir
+from concourse.masks import make_identity
+
+M, K, N = 512, 1024, 2048
+FLOPS = 3 * 2 * M * K * N
+F32 = mybir.dt.float32
+BF16 = mybir.dt.bfloat16
+U32 = mybir.dt.uint32
+I32 = mybir.dt.int32
+U8 = mybir.dt.uint8
+E4M3 = mybir.dt.float8_e4m3fn_x4
+E5M2 = mybir.dt.float8_e5m2_x4
+E2M1 = mybir.dt.float4_e2m1fn_x4
+MULT = mybir.AluOpType.mult
+SUB = mybir.AluOpType.subtract
+
+P = 128
+MT = M // P
+KG = K // 512
+NG = N // 512
+K_ENG = {0: 1, 1: 2, 2: 1, 3: 2, 4: 2, 6: 2}
+K_AT = {0: [4, 5], 1: [6, 7], 2: [8], 3: [9], 4: [10], 5: [11], 6: [12], 7: [13], 8: [14], 9: [15]}
+QK_AT = {1: (1, 0), 2: (1, 1), 4: (2, 0), 6: (2, 1), 8: (3, 0), 10: (3, 1)}
+N_AT = {b: [b - 1] for b in range(1, 11)} | {11: [10, 11], 12: [12, 13], 13: [14, 15]}
+QN_AT = {3: [(0, 0)], 5: [(0, 1)], 7: [(1, 0)], 9: [(1, 1)], 11: [(2, 0)], 12: [(2, 1)], 13: [(3, 0)], 14: [(3, 1)]}
+
+
+def tile_teacher_student_logits_s9_kernel(tc, u, gain, w, c, teacher_words, teacher_scales, zs_out, zt_out, du_out):
+    nc = tc.nc
+    with ExitStack() as ctx:
+        keep = ctx.enter_context(tc.tile_pool(name="keep", bufs=1))
+        work = ctx.enter_context(tc.tile_pool(name="work", bufs=3))
+        psum = ctx.enter_context(tc.psum_pool(name="psum", bufs=2))
+        ident = keep.tile([P, P], F32, name="ident", align_bytes=64)
+        ident_b = keep.tile([P, P], BF16, name="ident_b", align_bytes=64)
+        rows = keep.tile([P, 512], BF16, name="rows", align_bytes=64)
+        cg = keep.tile([P, 6, 4], BF16, name="cg", align_bytes=64)
+        gain_bc = keep.tile([P, KG * 512], BF16, name="gain_bc", align_bytes=64)
+        c_bc = keep.tile([P, NG * 512], BF16, name="c_bc", align_bytes=64)
+        x_codes = keep.tile([P, MT, KG * P], U32, name="x_codes", align_bytes=64)
+        x_scales = keep.tile([P, MT, KG * P], U8, name="x_scales", align_bytes=64)
+        t_words = keep.tile([P, KG, 2 * N], U8, name="t_words", align_bytes=64)
+        t_scales = keep.tile([P, KG, N], U8, name="t_scales", align_bytes=64)
+        w_raw = keep.tile([P, NG, KG, 4, 512], BF16, name="w_raw", align_bytes=64)
+        wk_codes = keep.tile([P, NG, KG, 512], U32, name="wk_codes", align_bytes=64)
+        wk_scales = keep.tile([P, NG, KG, 512], U8, name="wk_scales", align_bytes=64)
+        wn_codes = keep.tile([P, NG, KG, 512], U32, name="wn_codes", align_bytes=64)
+        wn_scales = keep.tile([P, NG, KG, 512], U8, name="wn_scales", align_bytes=64)
+        d_codes = keep.tile([P, NG, MT, P], U32, name="d_codes", align_bytes=64)
+        d_scales = keep.tile([P, NG, MT, P], U8, name="d_scales", align_bytes=64)
+        u_sb = keep.tile([P, MT, K], BF16, name="u_sb", align_bytes=64)
+
+        make_identity(nc, ident[:])
+        ctx.enter_context(tc.manual_schedule())
+        nc.vector.memset(rows[:], 0.0)
+        nc.vector.memset(t_scales[:].rearrange("p g n -> p (g n)").bitcast(I32), 0)
+        nc.scalar.dma_start(out=rows[0:4, :], in_=c.rearrange("(g n) -> g n", g=4))
+        nc.scalar.dma_start(out=rows[4:6, :], in_=gain.rearrange("(g n) -> g n", g=2))
+        nc.vector.tensor_copy(out=ident_b[:], in_=ident[:])
+
+        def load_u(m):
+            nc.sync.dma_start(out=u_sb[:, m, :], in_=u[m * P : (m + 1) * P, :])
+
+        def load_w(g, kg):
+            nc.sync.dma_start(
+                out=w_raw[:, g, kg, :, :],
+                in_=w[512 * kg : 512 * (kg + 1), 512 * g : 512 * (g + 1)].rearrange("(p j) n -> p j n", j=4),
+            )
+
+        def load_teacher(half):
+            cols = slice(half * N, (half + 1) * N)
+            nc.sync.dma_start(
+                out=t_words[:, :, cols].bitcast(I32),
+                in_=teacher_words.rearrange("g p n -> p g n")[:, :, cols].bitcast(I32),
+            )
+
+        def load_teacher_scales():
+            for q in range(4):
+                nc.sync.dma_start(
+                    out=t_scales[32 * q : 32 * q + 4, :, :].bitcast(I32),
+                    in_=teacher_scales[:, 4 * q : 4 * q + 4, :].rearrange("g r n -> r g n").bitcast(I32),
+                )
+
+        load_w(0, 0)
+        load_u(0)
+        load_w(0, 1)
+        load_u(1)
+        load_teacher_scales()
+        load_teacher(0)
+        load_u(2)
+        load_u(3)
+        load_w(1, 0)
+        load_w(1, 1)
+        load_teacher(1)
+        load_w(2, 0)
+        load_w(2, 1)
+        load_w(3, 0)
+        load_w(3, 1)
+
+        def make_cg():
+            ps = psum.tile([P, 4, P], BF16, name="ps_rows", tag="e")
+            for t in range(4):
+                nc.tensor.transpose(ps[:, t, :], rows[:, t:512:4], ident_b[:])
+            nc.vector.tensor_copy(out=cg[:], in_=ps[:, :, 0:6].rearrange("p t r -> p r t"))
+
+        def broadcast_rows(first, dst, tag):
+            ps = psum.tile([P, 2, 4, P], BF16, name="ps_bc", tag=tag)
+            for r in range(2):
+                for t in range(4):
+                    nc.tensor.transpose(ps[:, r, t, :], cg[:, first + r, t : t + 1].to_broadcast([P, P]), ident_b[:])
+            nc.scalar.copy(out=dst.rearrange("p (r q t) -> p r q t", r=2, t=4), in_=ps[:].rearrange("p r t q -> p r q t"))
+
+        x_bf = {}
+        x_grp = {}
+
+        def x_mul(m):
+            x_bf[m] = work.tile([P, K], BF16, name="x_bf", align_bytes=64)
+            nc.vector.tensor_tensor(out=x_bf[m][:], in0=u_sb[:, m, :], in1=gain_bc[:], op=MULT)
+
+        def x_turn(m, eng):
+            ps = psum.tile([P, KG * 2, P], F32, name="ps_x", tag="e")
+            words = x_bf[m][:].bitcast(F32)
+            for kg in range(KG):
+                for e in range(2):
+                    nc.tensor.transpose(ps[:, 2 * kg + e, :], words[:, 256 * kg + e : 256 * (kg + 1) : 2], ident[:])
+            x_grp[m] = work.tile([P, KG * P * 4], BF16, name="x_grp", align_bytes=64)
+            for_out = x_grp[m][:].bitcast(F32).rearrange("p (g m e) -> p g m e", g=KG, e=2)
+            for_in = ps[:].rearrange("p (g e) m -> p g m e", e=2)
+            if eng == 0:
+                nc.scalar.copy(out=for_out, in_=for_in)
+            else:
+                nc.vector.tensor_copy(out=for_out, in_=for_in)
+
+        def x_quant(m):
+            nc.vector.quantize_mx(out=x_codes[:, m, :].bitcast(E4M3), scales=x_scales[:, m, :], in_=x_grp[m][:])
+
+        wk_grp = {}
+        wn_grp = {}
+
+        def w_inter(g, kg, a, b, eng):
+            if (g, kg) not in wk_grp:
+                wk_grp[g, kg] = work.tile([P, 2048], BF16, name="wk_grp", align_bytes=64)
+            dst = wk_grp[g, kg][:, 4 * a : 4 * b].rearrange("p (n i j) -> p n j i", j=4, i=4)
+            src = w_raw[:, g, kg, :, a:b].rearrange("p j (n i) -> p n j i", i=4)
+            if eng == 0:
+                nc.scalar.copy(out=dst, in_=src)
+            elif eng == 2:
+                nc.gpsimd.tensor_scalar(out=dst, in0=src, scalar1=1.0, scalar2=0.0, op0=MULT, op1=mybir.AluOpType.add)
+            else:
+                nc.vector.tensor_copy(out=dst, in_=src)
+
+        def wk_quant(g, kg):
+            nc.vector.quantize_mx(out=wk_codes[:, g, kg, :].bitcast(E4M3), scales=wk_scales[:, g, kg, :], in_=wk_grp[g, kg][:])
+
+        def w_turn(g, kg, h):
+            ps = psum.tile([P, 4, P], F32, name="ps_w", tag="w")
+            for j in range(2):
+                words = w_raw[:, g, kg, 2 * h + j, :].bitcast(F32)
+                for e in range(2):
+                    nc.tensor.transpose(ps[:, 2 * j + e, :], words[:, e:256:2], ident[:])
+            return ps
+
+        def w_out(g, kg, h, ps):
+            if (g, kg) not in wn_grp:
+                wn_grp[g, kg] = work.tile([P, 2048], BF16, name="wn_grp", align_bytes=64)
+            dst = wn_grp[g, kg][:].bitcast(F32)[:, 512 * h : 512 * (h + 1)]
+            nc.scalar.copy(
+                out=dst.rearrange("q (j p e) -> q j p e", j=2, e=2), in_=ps[:].rearrange("q (j e) p -> q j p e", e=2)
+            )
+
+        def wn_quant(g, kg):
+            nc.vector.quantize_mx(out=wn_codes[:, g, kg, :].bitcast(E4M3), scales=wn_scales[:, g, kg, :], in_=wn_grp[g, kg][:])
+
+        def mx_student(g, m):
+            ps = psum.tile([P, 512], F32, name="ps_s", tag="s")
+            for kg in range(KG):
+                nc.tensor.matmul_mx(
+                    out=ps[:],
+                    lhsT=x_codes[:, m, kg * P : (kg + 1) * P].bitcast(E4M3),
+                    lhsT_scale=x_scales[:, m, kg * P : (kg + 1) * P],
+                    rhs=wk_codes[:, g, kg, :].bitcast(E4M3),
+                    rhs_scale=wk_scales[:, g, kg, :],
+                    start=(kg == 0),
+                    stop=(kg == KG - 1),
+                )
+            return ps
+
+        def mx_teacher(g, m):
+            ps = psum.tile([P, 512], F32, name="ps_t", tag="t")
+            for kg in range(KG):
+                nc.tensor.matmul_mx(
+                    out=ps[:],
+                    lhsT=x_codes[:, m, kg * P : (kg + 1) * P].bitcast(E4M3),
+                    lhsT_scale=x_scales[:, m, kg * P : (kg + 1) * P],
+                    rhs=t_words[:, kg, 1024 * g : 1024 * (g + 1)].bitcast(E2M1),
+                    rhs_scale=t_scales[:, kg, 512 * g : 512 * (g + 1)],
+                    start=(kg == 0),
+                    stop=(kg == KG - 1),
+                )
+            return ps
+
+        zs = {}
+        zt = {}
+        es = {}
+        eps = {}
+        dg = {}
+
+        def out_slice(o, g, m):
+            return o[m * P : (m + 1) * P, 512 * g : 512 * (g + 1)]
+
+        def do_zt(b, ps):
+            g, m = divmod(b, MT)
+            zt[b] = work.tile([P, 512], F32, name="zt", bufs=6)
+            nc.scalar.copy(out=zt[b][:], in_=ps[:])
+            nc.sync.dma_start(out=out_slice(zt_out, g, m), in_=zt[b][:])
+
+        def do_zs(b, ps):
+            g, m = divmod(b, MT)
+            zs[b] = work.tile([P, 512], F32, name="zs", bufs=6)
+            nc.vector.tensor_tensor(out=zs[b][:], in0=ps[:], in1=c_bc[:, 512 * g : 512 * (g + 1)], op=MULT)
+            nc.sync.dma_start(out=out_slice(zs_out, g, m), in_=zs[b][:])
+
+        def do_e(b):
+            es[b] = work.tile([P, 4, P], F32, name="es", bufs=3)
+            nc.vector.tensor_tensor(
+                out=es[b][:],
+                in0=zs[b][:].rearrange("m (q t) -> m t q", t=4),
+                in1=zt[b][:].rearrange("m (q t) -> m t q", t=4),
+                op=SUB,
+            )
+
+        def e_turn(b):
+            eps[b] = psum.tile([P, 4, P], F32, name="ps_e", tag="e")
+            for t in range(4):
+                nc.tensor.transpose(eps[b][:, t, :], es[b][:, t, :], ident[:])
+
+        def do_d(b):
+            g = b // MT
+            dg[b] = work.tile([P, P, 4], BF16, name="dg", align_bytes=64)
+            nc.vector.tensor_tensor(
+                out=dg[b][:],
+                in0=eps[b][:].rearrange("q t m -> q m t"),
+                in1=cg[:, g : g + 1, :].to_broadcast([P, P, 4]),
+                op=MULT,
+            )
+
+        def d_quant(b):
+            g, m = divmod(b, MT)
+            nc.vector.quantize_mx(
+                out=d_codes[:, g, m, :].bitcast(E5M2),
+                scales=d_scales[:, g, m, :],
+                in_=dg[b][:].rearrange("p m t -> p (m t)"),
+            )
+
+        dx = {}
+
+        def mx_back(m, kg, groups, tag):
+            if (m, kg) not in dx:
+                dx[m, kg] = psum.tile([P, 512], F32, name="ps_dx", tag=tag)
+            for g in groups:
+                nc.tensor.matmul_mx(
+                    out=dx[m, kg][:],
+                    lhsT=d_codes[:, g, m, :].bitcast(E5M2),
+                    lhsT_scale=d_scales[:, g, m, :],
+                    rhs=wn_codes[:, g, kg, :].bitcast(E4M3),
+                    rhs_scale=wn_scales[:, g, kg, :],
+                    start=(g == 0),
+                    stop=(g == NG - 1),
+                )
+
+        def do_du(m, kg):
+            du = work.tile([P, 512], F32, name="du", bufs=8)
+            nc.vector.tensor_tensor(
+                out=du[:].rearrange("m (p j) -> m p j", j=4),
+                in0=dx[m, kg][:].rearrange("m (j p) -> m p j", j=4),
+                in1=gain_bc[:, 512 * kg : 512 * (kg + 1)].rearrange("m (p j) -> m p j", j=4),
+                op=MULT,
+            )
+            nc.sync.dma_start(out=du_out[m * P : (m + 1) * P, 512 * kg : 512 * (kg + 1)], in_=du[:])
+
+        def chunk(k):
+            g, rest = divmod(k, 4)
+            kg, h = divmod(rest, 2)
+            return g, kg, h
+
+        def prep_k(k):
+            g, kg, h = chunk(k)
+            w_inter(g, kg, 256 * h, 256 * h + 256, K_ENG.get(k, 0))
+
+        def prep_n(k):
+            g, kg, h = chunk(k)
+            w_out(g, kg, h, w_turn(g, kg, h))
+
+        make_cg()
+        broadcast_rows(4, gain_bc[:], "w")
+        prep_k(0)
+        prep_k(1)
+        x_mul(0)
+        x_turn(0, 0)
+        broadcast_rows(0, c_bc[:, 0:1024], "t")
+        prep_k(2)
+        prep_k(3)
+        x_quant(0)
+        wk_quant(0, 0)
+        wk_quant(0, 1)
+        x_mul(1)
+        x_mul(2)
+
+        for b in range(16):
+            g, m = divmod(b, MT)
+            ps_s = mx_student(g, m)
+            ps_t = mx_teacher(g, m)
+            do_zt(b, ps_t)
+            do_zs(b, ps_s)
+            if b == 0:
+                x_turn(1, 0)
+                x_turn(2, 0)
+                x_mul(3)
+            if b == 1:
+                x_turn(3, 0)
+            if b < 3:
+                x_quant(b + 1)
+            if b == 2:
+                broadcast_rows(2, c_bc[:, 1024:2048], "t")
+            if b >= 2:
+                e_turn(b - 2)
+                do_d(b - 2)
+            for k in K_AT.get(b, []):
+                prep_k(k)
+            for k in N_AT.get(b, []):
+                prep_n(k)
+            if b in QK_AT:
+                wk_quant(*QK_AT[b])
+            do_e(b)
+            if b >= 2:
+                d_quant(b - 2)
+            if b in QN_AT:
+                for a in QN_AT[b]:
+                    wn_quant(*a)
+            if b == 14:
+                mx_back(0, 0, (0, 1, 2), "w")
+                mx_back(0, 1, (0, 1, 2), "w")
+            if b == 15:
+                mx_back(0, 0, (3,), "w")
+                mx_back(0, 1, (3,), "w")
+
+        e_turn(14)
+        do_d(14)
+        do_du(0, 0)
+        d_quant(14)
+        mx_back(1, 0, (0, 1, 2), "s")
+        mx_back(1, 1, (0, 1, 2), "s")
+        e_turn(15)
+        do_d(15)
+        do_du(0, 1)
+        d_quant(15)
+        mx_back(1, 0, (3,), "s")
+        mx_back(1, 1, (3,), "s")
+        do_du(1, 0)
+        do_du(1, 1)
+        for kg in range(KG):
+            mx_back(2, kg, (0, 1, 2, 3), "t")
+            do_du(2, kg)
+        for kg in range(KG):
+            mx_back(3, kg, (0, 1, 2, 3), "w")
+            do_du(3, kg)

@@ -20,11 +20,11 @@ P = 128
 MT = M // P
 KG = K // 512
 NG = N // 512
-K_ENG = {0: 1, 1: 2, 2: 1, 3: 2, 4: 2, 6: 2}
-K_AT = {0: [4, 5], 1: [6, 7], 2: [8], 3: [9], 4: [10], 5: [11], 6: [12], 7: [13], 8: [14], 9: [15]}
-QK_AT = {1: (1, 0), 2: (1, 1), 4: (2, 0), 6: (2, 1), 8: (3, 0), 10: (3, 1)}
-N_AT = {b: [b - 1] for b in range(1, 11)} | {11: [10, 11], 12: [12, 13], 13: [14, 15]}
-QN_AT = {3: [(0, 0)], 5: [(0, 1)], 7: [(1, 0)], 9: [(1, 1)], 11: [(2, 0)], 12: [(2, 1)], 13: [(3, 0)], 14: [(3, 1)]}
+K_ENG = {0: 1, 1: 1, 2: 1}
+K_AT = {0: [4, 5, 6, 7], 1: [8, 9], 2: [10, 11], 3: [12, 13], 4: [14, 15]}
+QK_AT = {0: [(1, 0)], 1: [(1, 1)], 2: [(2, 0)], 3: [(2, 1)], 4: [(3, 0)], 5: [(3, 1)]}
+N_AT = {0: [4], 1: [5], 2: [6, 7], 3: [8, 9], 4: [10, 11], 5: [12, 13], 6: [14, 15]}
+QN_AT = {2: [(1, 0)], 3: [(1, 1)], 4: [(2, 0)], 5: [(2, 1)], 6: [(3, 0)], 7: [(3, 1)]}
 
 
 def tile_teacher_student_logits_s9_kernel(tc, u, gain, w, c, teacher_words, teacher_scales, zs_out, zt_out, du_out):
@@ -53,7 +53,6 @@ def tile_teacher_student_logits_s9_kernel(tc, u, gain, w, c, teacher_words, teac
         u_sb = keep.tile([P, MT, K], BF16, name="u_sb", align_bytes=64)
 
         make_identity(nc, ident[:])
-        ctx.enter_context(tc.manual_schedule())
         nc.vector.memset(rows[:], 0.0)
         nc.vector.memset(t_scales[:].rearrange("p g n -> p (g n)").bitcast(I32), 0)
         nc.scalar.dma_start(out=rows[0:4, :], in_=c.rearrange("(g n) -> g n", g=4))
@@ -204,6 +203,7 @@ def tile_teacher_student_logits_s9_kernel(tc, u, gain, w, c, teacher_words, teac
         zs = {}
         zt = {}
         es = {}
+        dp = {}
         eps = {}
         dg = {}
 
@@ -223,35 +223,39 @@ def tile_teacher_student_logits_s9_kernel(tc, u, gain, w, c, teacher_words, teac
             nc.sync.dma_start(out=out_slice(zs_out, g, m), in_=zs[b][:])
 
         def do_e(b):
-            es[b] = work.tile([P, 4, P], F32, name="es", bufs=3)
-            nc.vector.tensor_tensor(
-                out=es[b][:],
-                in0=zs[b][:].rearrange("m (q t) -> m t q", t=4),
-                in1=zt[b][:].rearrange("m (q t) -> m t q", t=4),
-                op=SUB,
-            )
+            es[b] = work.tile([P, 512], F32, name="es", bufs=4)
+            nc.vector.tensor_tensor(out=es[b][:], in0=zs[b][:], in1=zt[b][:], op=SUB)
 
-        def e_turn(b):
-            eps[b] = psum.tile([P, 4, P], F32, name="ps_e", tag="e")
-            for t in range(4):
-                nc.tensor.transpose(eps[b][:, t, :], es[b][:, t, :], ident[:])
-
-        def do_d(b):
+        def do_d(b, eng):
             g = b // MT
-            dg[b] = work.tile([P, P, 4], BF16, name="dg", align_bytes=64)
-            nc.vector.tensor_tensor(
-                out=dg[b][:],
-                in0=eps[b][:].rearrange("q t m -> q m t"),
-                in1=cg[:, g : g + 1, :].to_broadcast([P, P, 4]),
+            dp[b] = work.tile([P, 512], BF16, name="dp", bufs=4, align_bytes=64)
+            eng.tensor_tensor(
+                out=dp[b][:].rearrange("m (u p e) -> m p u e", u=2, e=2),
+                in0=es[b][:].rearrange("m (p u e) -> m p u e", u=2, e=2),
+                in1=c_bc[:, 512 * g : 512 * (g + 1)].rearrange("m (p u e) -> m p u e", u=2, e=2),
                 op=MULT,
             )
 
-        def d_quant(b):
-            g, m = divmod(b, MT)
+        def d_turn(i):
+            eps[i] = psum.tile([P, 4, P], F32, name="ps_e", tag="e")
+            for b in (0, 1):
+                words = dp[2 * i + b][:].bitcast(F32)
+                for half in range(2):
+                    nc.tensor.transpose(eps[i][:, 2 * b + half, :], words[:, P * half : P * (half + 1)], ident[:])
+
+        def d_out(i):
+            dg[i] = work.tile([P, 2 * P * 4], BF16, name="dg", align_bytes=64)
+            nc.scalar.copy(
+                out=dg[i][:].bitcast(F32).rearrange("p (b m u) -> p b m u", b=2, u=2),
+                in_=eps[i][:].rearrange("p (b u) m -> p b m u", u=2),
+            )
+
+        def d_quant(i):
+            g, m = divmod(2 * i, MT)
             nc.vector.quantize_mx(
-                out=d_codes[:, g, m, :].bitcast(E5M2),
-                scales=d_scales[:, g, m, :],
-                in_=dg[b][:].rearrange("p m t -> p (m t)"),
+                out=d_codes[:, g, m : m + 2, :].rearrange("p m n -> p (m n)").bitcast(E5M2),
+                scales=d_scales[:, g, m : m + 2, :].rearrange("p m n -> p (m n)"),
+                in_=dg[i][:],
             )
 
         dx = {}
@@ -296,68 +300,72 @@ def tile_teacher_student_logits_s9_kernel(tc, u, gain, w, c, teacher_words, teac
         make_cg()
         broadcast_rows(4, gain_bc[:], "w")
         prep_k(0)
-        prep_k(1)
         x_mul(0)
         x_turn(0, 0)
-        broadcast_rows(0, c_bc[:, 0:1024], "t")
+        prep_k(1)
         prep_k(2)
         prep_k(3)
+        prep_n(0)
+        x_mul(1)
         x_quant(0)
         wk_quant(0, 0)
+        prep_n(1)
+        x_turn(1, 0)
         wk_quant(0, 1)
-        x_mul(1)
+        broadcast_rows(0, c_bc[:, 0:1024], "e")
+        x_quant(1)
         x_mul(2)
 
-        for b in range(16):
-            g, m = divmod(b, MT)
-            ps_s = mx_student(g, m)
-            ps_t = mx_teacher(g, m)
-            do_zt(b, ps_t)
-            do_zs(b, ps_s)
-            if b == 0:
-                x_turn(1, 0)
-                x_turn(2, 0)
-                x_mul(3)
-            if b == 1:
-                x_turn(3, 0)
-            if b < 3:
-                x_quant(b + 1)
-            if b == 2:
-                broadcast_rows(2, c_bc[:, 1024:2048], "t")
-            if b >= 2:
-                e_turn(b - 2)
-                do_d(b - 2)
-            for k in K_AT.get(b, []):
+        for i in range(8):
+            pair = (2 * i, 2 * i + 1)
+            for b in pair:
+                g, m = divmod(b, MT)
+                ps_s = mx_student(g, m)
+                ps_t = mx_teacher(g, m)
+                do_zt(b, ps_t)
+                do_zs(b, ps_s)
+                if b == 0:
+                    prep_n(2)
+                    prep_n(3)
+                    x_turn(2, 0)
+                    x_mul(3)
+                    wn_quant(0, 0)
+                if b == 1:
+                    x_turn(3, 0)
+                    x_quant(2)
+                    wn_quant(0, 1)
+                    broadcast_rows(2, c_bc[:, 1024:2048], "e")
+                    x_quant(3)
+            if i >= 1:
+                d_turn(i - 1)
+                d_out(i - 1)
+            do_e(pair[0])
+            do_e(pair[1])
+            for k in K_AT.get(i, []):
                 prep_k(k)
-            for k in N_AT.get(b, []):
+            for k in N_AT.get(i, []):
                 prep_n(k)
-            if b in QK_AT:
-                wk_quant(*QK_AT[b])
-            do_e(b)
-            if b >= 2:
-                d_quant(b - 2)
-            if b in QN_AT:
-                for a in QN_AT[b]:
-                    wn_quant(*a)
-            if b == 14:
+            for a in QK_AT.get(i, []):
+                wk_quant(*a)
+            do_d(pair[0], nc.vector)
+            do_d(pair[1], nc.vector)
+            if i >= 1:
+                d_quant(i - 1)
+            for a in QN_AT.get(i, []):
+                wn_quant(*a)
+            if i == 6:
                 mx_back(0, 0, (0, 1, 2), "w")
                 mx_back(0, 1, (0, 1, 2), "w")
-            if b == 15:
-                mx_back(0, 0, (3,), "w")
-                mx_back(0, 1, (3,), "w")
 
-        e_turn(14)
-        do_d(14)
+        d_turn(7)
+        d_out(7)
+        mx_back(0, 0, (3,), "w")
+        mx_back(0, 1, (3,), "w")
+        mx_back(1, 0, (0, 1, 2, 3), "s")
+        mx_back(1, 1, (0, 1, 2, 3), "s")
         do_du(0, 0)
-        d_quant(14)
-        mx_back(1, 0, (0, 1, 2), "s")
-        mx_back(1, 1, (0, 1, 2), "s")
-        e_turn(15)
-        do_d(15)
+        d_quant(7)
         do_du(0, 1)
-        d_quant(15)
-        mx_back(1, 0, (3,), "s")
-        mx_back(1, 1, (3,), "s")
         do_du(1, 0)
         do_du(1, 1)
         for kg in range(KG):

from contextlib import ExitStack

import concourse.mybir as mybir
from concourse.masks import make_identity

M, K, N = 512, 1024, 2048
FLOPS = 3 * 2 * M * K * N
F32 = mybir.dt.float32
BF16 = mybir.dt.bfloat16
U32 = mybir.dt.uint32
I32 = mybir.dt.int32
U8 = mybir.dt.uint8
E4M3 = mybir.dt.float8_e4m3fn_x4
E5M2 = mybir.dt.float8_e5m2_x4
E2M1 = mybir.dt.float4_e2m1fn_x4
MULT = mybir.AluOpType.mult
SUB = mybir.AluOpType.subtract

P = 128
MT = M // P
KG = K // 512
NG = N // 512
K_ENG = {0: 1, 1: 1, 2: 1}
K_AT = {0: [4, 5, 6, 7], 1: [8, 9], 2: [10, 11], 3: [12, 13], 4: [14, 15]}
QK_AT = {0: [(1, 0)], 1: [(1, 1)], 2: [(2, 0)], 3: [(2, 1)], 4: [(3, 0)], 5: [(3, 1)]}
N_AT = {0: [4], 1: [5], 2: [6, 7], 3: [8, 9], 4: [10, 11], 5: [12, 13], 6: [14, 15]}
QN_AT = {2: [(1, 0)], 3: [(1, 1)], 4: [(2, 0)], 5: [(2, 1)], 6: [(3, 0)], 7: [(3, 1)]}


def tile_teacher_student_logits_s9_kernel(tc, u, gain, w, c, teacher_words, teacher_scales, zs_out, zt_out, du_out):
    nc = tc.nc
    with ExitStack() as ctx:
        keep = ctx.enter_context(tc.tile_pool(name="keep", bufs=1))
        work = ctx.enter_context(tc.tile_pool(name="work", bufs=3))
        psum = ctx.enter_context(tc.psum_pool(name="psum", bufs=2))
        ident = keep.tile([P, P], F32, name="ident", align_bytes=64)
        ident_b = keep.tile([P, P], BF16, name="ident_b", align_bytes=64)
        rows = keep.tile([P, 512], BF16, name="rows", align_bytes=64)
        cg = keep.tile([P, 6, 4], BF16, name="cg", align_bytes=64)
        gain_bc = keep.tile([P, KG * 512], BF16, name="gain_bc", align_bytes=64)
        c_bc = keep.tile([P, NG * 512], BF16, name="c_bc", align_bytes=64)
        x_codes = keep.tile([P, MT, KG * P], U32, name="x_codes", align_bytes=64)
        x_scales = keep.tile([P, MT, KG * P], U8, name="x_scales", align_bytes=64)
        t_words = keep.tile([P, KG, 2 * N], U8, name="t_words", align_bytes=64)
        t_scales = keep.tile([P, KG, N], U8, name="t_scales", align_bytes=64)
        w_raw = keep.tile([P, NG, KG, 4, 512], BF16, name="w_raw", align_bytes=64)
        wk_codes = keep.tile([P, NG, KG, 512], U32, name="wk_codes", align_bytes=64)
        wk_scales = keep.tile([P, NG, KG, 512], U8, name="wk_scales", align_bytes=64)
        wn_codes = keep.tile([P, NG, KG, 512], U32, name="wn_codes", align_bytes=64)
        wn_scales = keep.tile([P, NG, KG, 512], U8, name="wn_scales", align_bytes=64)
        d_codes = keep.tile([P, NG, MT, P], U32, name="d_codes", align_bytes=64)
        d_scales = keep.tile([P, NG, MT, P], U8, name="d_scales", align_bytes=64)
        u_sb = keep.tile([P, MT, K], BF16, name="u_sb", align_bytes=64)

        make_identity(nc, ident[:])
        nc.vector.memset(rows[:], 0.0)
        nc.vector.memset(t_scales[:].rearrange("p g n -> p (g n)").bitcast(I32), 0)
        nc.scalar.dma_start(out=rows[0:4, :], in_=c.rearrange("(g n) -> g n", g=4))
        nc.scalar.dma_start(out=rows[4:6, :], in_=gain.rearrange("(g n) -> g n", g=2))
        nc.vector.tensor_copy(out=ident_b[:], in_=ident[:])

        def load_u(m):
            nc.sync.dma_start(out=u_sb[:, m, :], in_=u[m * P : (m + 1) * P, :])

        def load_w(g, kg):
            nc.sync.dma_start(
                out=w_raw[:, g, kg, :, :],
                in_=w[512 * kg : 512 * (kg + 1), 512 * g : 512 * (g + 1)].rearrange("(p j) n -> p j n", j=4),
            )

        def load_teacher(half):
            cols = slice(half * N, (half + 1) * N)
            nc.sync.dma_start(
                out=t_words[:, :, cols].bitcast(I32),
                in_=teacher_words.rearrange("g p n -> p g n")[:, :, cols].bitcast(I32),
            )

        def load_teacher_scales():
            for q in range(4):
                nc.sync.dma_start(
                    out=t_scales[32 * q : 32 * q + 4, :, :].bitcast(I32),
                    in_=teacher_scales[:, 4 * q : 4 * q + 4, :].rearrange("g r n -> r g n").bitcast(I32),
                )

        load_w(0, 0)
        load_u(0)
        load_w(0, 1)
        load_u(1)
        load_teacher_scales()
        load_teacher(0)
        load_u(2)
        load_u(3)
        load_w(1, 0)
        load_w(1, 1)
        load_teacher(1)
        load_w(2, 0)
        load_w(2, 1)
        load_w(3, 0)
        load_w(3, 1)

        def make_cg():
            ps = psum.tile([P, 4, P], BF16, name="ps_rows", tag="e")
            for t in range(4):
                nc.tensor.transpose(ps[:, t, :], rows[:, t:512:4], ident_b[:])
            nc.vector.tensor_copy(out=cg[:], in_=ps[:, :, 0:6].rearrange("p t r -> p r t"))

        def broadcast_rows(first, dst, tag):
            ps = psum.tile([P, 2, 4, P], BF16, name="ps_bc", tag=tag)
            for r in range(2):
                for t in range(4):
                    nc.tensor.transpose(ps[:, r, t, :], cg[:, first + r, t : t + 1].to_broadcast([P, P]), ident_b[:])
            nc.scalar.copy(out=dst.rearrange("p (r q t) -> p r q t", r=2, t=4), in_=ps[:].rearrange("p r t q -> p r q t"))

        x_bf = {}
        x_grp = {}

        def x_mul(m):
            x_bf[m] = work.tile([P, K], BF16, name="x_bf", align_bytes=64)
            nc.vector.tensor_tensor(out=x_bf[m][:], in0=u_sb[:, m, :], in1=gain_bc[:], op=MULT)

        def x_turn(m, eng):
            ps = psum.tile([P, KG * 2, P], F32, name="ps_x", tag="e")
            words = x_bf[m][:].bitcast(F32)
            for kg in range(KG):
                for e in range(2):
                    nc.tensor.transpose(ps[:, 2 * kg + e, :], words[:, 256 * kg + e : 256 * (kg + 1) : 2], ident[:])
            x_grp[m] = work.tile([P, KG * P * 4], BF16, name="x_grp", align_bytes=64)
            for_out = x_grp[m][:].bitcast(F32).rearrange("p (g m e) -> p g m e", g=KG, e=2)
            for_in = ps[:].rearrange("p (g e) m -> p g m e", e=2)
            if eng == 0:
                nc.scalar.copy(out=for_out, in_=for_in)
            else:
                nc.vector.tensor_copy(out=for_out, in_=for_in)

        def x_quant(m):
            nc.vector.quantize_mx(out=x_codes[:, m, :].bitcast(E4M3), scales=x_scales[:, m, :], in_=x_grp[m][:])

        wk_grp = {}
        wn_grp = {}

        def w_inter(g, kg, a, b, eng):
            if (g, kg) not in wk_grp:
                wk_grp[g, kg] = work.tile([P, 2048], BF16, name="wk_grp", align_bytes=64)
            dst = wk_grp[g, kg][:, 4 * a : 4 * b].rearrange("p (n i j) -> p n j i", j=4, i=4)
            src = w_raw[:, g, kg, :, a:b].rearrange("p j (n i) -> p n j i", i=4)
            if eng == 0:
                nc.scalar.copy(out=dst, in_=src)
            elif eng == 2:
                nc.gpsimd.tensor_scalar(out=dst, in0=src, scalar1=1.0, scalar2=0.0, op0=MULT, op1=mybir.AluOpType.add)
            else:
                nc.vector.tensor_copy(out=dst, in_=src)

        def wk_quant(g, kg):
            nc.vector.quantize_mx(out=wk_codes[:, g, kg, :].bitcast(E4M3), scales=wk_scales[:, g, kg, :], in_=wk_grp[g, kg][:])

        def w_turn(g, kg, h):
            ps = psum.tile([P, 4, P], F32, name="ps_w", tag="w")
            for j in range(2):
                words = w_raw[:, g, kg, 2 * h + j, :].bitcast(F32)
                for e in range(2):
                    nc.tensor.transpose(ps[:, 2 * j + e, :], words[:, e:256:2], ident[:])
            return ps

        def w_out(g, kg, h, ps):
            if (g, kg) not in wn_grp:
                wn_grp[g, kg] = work.tile([P, 2048], BF16, name="wn_grp", align_bytes=64)
            dst = wn_grp[g, kg][:].bitcast(F32)[:, 512 * h : 512 * (h + 1)]
            nc.scalar.copy(
                out=dst.rearrange("q (j p e) -> q j p e", j=2, e=2), in_=ps[:].rearrange("q (j e) p -> q j p e", e=2)
            )

        def wn_quant(g, kg):
            nc.vector.quantize_mx(out=wn_codes[:, g, kg, :].bitcast(E4M3), scales=wn_scales[:, g, kg, :], in_=wn_grp[g, kg][:])

        def mx_student(g, m):
            ps = psum.tile([P, 512], F32, name="ps_s", tag="s")
            for kg in range(KG):
                nc.tensor.matmul_mx(
                    out=ps[:],
                    lhsT=x_codes[:, m, kg * P : (kg + 1) * P].bitcast(E4M3),
                    lhsT_scale=x_scales[:, m, kg * P : (kg + 1) * P],
                    rhs=wk_codes[:, g, kg, :].bitcast(E4M3),
                    rhs_scale=wk_scales[:, g, kg, :],
                    start=(kg == 0),
                    stop=(kg == KG - 1),
                )
            return ps

        def mx_teacher(g, m):
            ps = psum.tile([P, 512], F32, name="ps_t", tag="t")
            for kg in range(KG):
                nc.tensor.matmul_mx(
                    out=ps[:],
                    lhsT=x_codes[:, m, kg * P : (kg + 1) * P].bitcast(E4M3),
                    lhsT_scale=x_scales[:, m, kg * P : (kg + 1) * P],
                    rhs=t_words[:, kg, 1024 * g : 1024 * (g + 1)].bitcast(E2M1),
                    rhs_scale=t_scales[:, kg, 512 * g : 512 * (g + 1)],
                    start=(kg == 0),
                    stop=(kg == KG - 1),
                )
            return ps

        zs = {}
        zt = {}
        es = {}
        dp = {}
        eps = {}
        dg = {}

        def out_slice(o, g, m):
            return o[m * P : (m + 1) * P, 512 * g : 512 * (g + 1)]

        def do_zt(b, ps):
            g, m = divmod(b, MT)
            zt[b] = work.tile([P, 512], F32, name="zt", bufs=6)
            nc.scalar.copy(out=zt[b][:], in_=ps[:])
            nc.sync.dma_start(out=out_slice(zt_out, g, m), in_=zt[b][:])

        def do_zs(b, ps):
            g, m = divmod(b, MT)
            zs[b] = work.tile([P, 512], F32, name="zs", bufs=6)
            nc.vector.tensor_tensor(out=zs[b][:], in0=ps[:], in1=c_bc[:, 512 * g : 512 * (g + 1)], op=MULT)
            nc.sync.dma_start(out=out_slice(zs_out, g, m), in_=zs[b][:])

        def do_e(b):
            es[b] = work.tile([P, 512], F32, name="es", bufs=4)
            nc.vector.tensor_tensor(out=es[b][:], in0=zs[b][:], in1=zt[b][:], op=SUB)

        def do_d(b, eng):
            g = b // MT
            dp[b] = work.tile([P, 512], BF16, name="dp", bufs=4, align_bytes=64)
            eng.tensor_tensor(
                out=dp[b][:].rearrange("m (u p e) -> m p u e", u=2, e=2),
                in0=es[b][:].rearrange("m (p u e) -> m p u e", u=2, e=2),
                in1=c_bc[:, 512 * g : 512 * (g + 1)].rearrange("m (p u e) -> m p u e", u=2, e=2),
                op=MULT,
            )

        def d_turn(i):
            eps[i] = psum.tile([P, 4, P], F32, name="ps_e", tag="e")
            for b in (0, 1):
                words = dp[2 * i + b][:].bitcast(F32)
                for half in range(2):
                    nc.tensor.transpose(eps[i][:, 2 * b + half, :], words[:, P * half : P * (half + 1)], ident[:])

        def d_out(i):
            dg[i] = work.tile([P, 2 * P * 4], BF16, name="dg", align_bytes=64)
            nc.scalar.copy(
                out=dg[i][:].bitcast(F32).rearrange("p (b m u) -> p b m u", b=2, u=2),
                in_=eps[i][:].rearrange("p (b u) m -> p b m u", u=2),
            )

        def d_quant(i):
            g, m = divmod(2 * i, MT)
            nc.vector.quantize_mx(
                out=d_codes[:, g, m : m + 2, :].rearrange("p m n -> p (m n)").bitcast(E5M2),
                scales=d_scales[:, g, m : m + 2, :].rearrange("p m n -> p (m n)"),
                in_=dg[i][:],
            )

        dx = {}

        def mx_back(m, kg, groups, tag):
            if (m, kg) not in dx:
                dx[m, kg] = psum.tile([P, 512], F32, name="ps_dx", tag=tag)
            for g in groups:
                nc.tensor.matmul_mx(
                    out=dx[m, kg][:],
                    lhsT=d_codes[:, g, m, :].bitcast(E5M2),
                    lhsT_scale=d_scales[:, g, m, :],
                    rhs=wn_codes[:, g, kg, :].bitcast(E4M3),
                    rhs_scale=wn_scales[:, g, kg, :],
                    start=(g == 0),
                    stop=(g == NG - 1),
                )

        def do_du(m, kg):
            du = work.tile([P, 512], F32, name="du", bufs=8)
            nc.vector.tensor_tensor(
                out=du[:].rearrange("m (p j) -> m p j", j=4),
                in0=dx[m, kg][:].rearrange("m (j p) -> m p j", j=4),
                in1=gain_bc[:, 512 * kg : 512 * (kg + 1)].rearrange("m (p j) -> m p j", j=4),
                op=MULT,
            )
            nc.sync.dma_start(out=du_out[m * P : (m + 1) * P, 512 * kg : 512 * (kg + 1)], in_=du[:])

        def chunk(k):
            g, rest = divmod(k, 4)
            kg, h = divmod(rest, 2)
            return g, kg, h

        def prep_k(k):
            g, kg, h = chunk(k)
            w_inter(g, kg, 256 * h, 256 * h + 256, K_ENG.get(k, 0))

        def prep_n(k):
            g, kg, h = chunk(k)
            w_out(g, kg, h, w_turn(g, kg, h))

        make_cg()
        broadcast_rows(4, gain_bc[:], "w")
        prep_k(0)
        x_mul(0)
        x_turn(0, 0)
        prep_k(1)
        prep_k(2)
        prep_k(3)
        prep_n(0)
        x_mul(1)
        x_quant(0)
        wk_quant(0, 0)
        prep_n(1)
        x_turn(1, 0)
        wk_quant(0, 1)
        broadcast_rows(0, c_bc[:, 0:1024], "e")
        x_quant(1)
        x_mul(2)

        for i in range(8):
            pair = (2 * i, 2 * i + 1)
            for b in pair:
                g, m = divmod(b, MT)
                ps_s = mx_student(g, m)
                ps_t = mx_teacher(g, m)
                do_zt(b, ps_t)
                do_zs(b, ps_s)
                if b == 0:
                    prep_n(2)
                    prep_n(3)
                    x_turn(2, 0)
                    x_mul(3)
                    wn_quant(0, 0)
                if b == 1:
                    x_turn(3, 0)
                    x_quant(2)
                    wn_quant(0, 1)
                    broadcast_rows(2, c_bc[:, 1024:2048], "e")
                    x_quant(3)
            if i >= 1:
                d_turn(i - 1)
                d_out(i - 1)
            do_e(pair[0])
            do_e(pair[1])
            for k in K_AT.get(i, []):
                prep_k(k)
            for k in N_AT.get(i, []):
                prep_n(k)
            for a in QK_AT.get(i, []):
                wk_quant(*a)
            do_d(pair[0], nc.vector)
            do_d(pair[1], nc.vector)
            if i >= 1:
                d_quant(i - 1)
            for a in QN_AT.get(i, []):
                wn_quant(*a)
            if i == 6:
                mx_back(0, 0, (0, 1, 2), "w")
                mx_back(0, 1, (0, 1, 2), "w")

        d_turn(7)
        d_out(7)
        mx_back(0, 0, (3,), "w")
        mx_back(0, 1, (3,), "w")
        mx_back(1, 0, (0, 1, 2, 3), "s")
        mx_back(1, 1, (0, 1, 2, 3), "s")
        do_du(0, 0)
        d_quant(7)
        do_du(0, 1)
        do_du(1, 0)
        do_du(1, 1)
        for kg in range(KG):
            mx_back(2, kg, (0, 1, 2, 3), "t")
            do_du(2, kg)
        for kg in range(KG):
            mx_back(3, kg, (0, 1, 2, 3), "w")
            do_du(3, kg)
